import numpy as np
import ml_dtypes


def mxq(x, axis, fmt="e4m3"):
    dtype, down = {"e4m3": (ml_dtypes.float8_e4m3fn, 7), "e5m2": (ml_dtypes.float8_e5m2, 14)}[fmt]
    v = np.moveaxis(np.asarray(x, np.float32).astype(ml_dtypes.bfloat16).astype(np.float64), axis, -1)
    blocks = v.reshape(v.shape[:-1] + (-1, 32))
    amax = np.abs(blocks).max(-1, keepdims=True)
    byte = np.maximum(np.where(amax > 0, np.frexp(amax)[1] - 1 + 127, 0) - down, 1)
    scale = np.exp2(byte - 127.0)
    codes = (blocks / scale).astype(np.float32).astype(dtype).astype(np.float64)
    return np.moveaxis((codes * scale).reshape(v.shape), -1, axis)


WIDE = False


def mx_kscale(k):
    if not WIDE:
        return np.ones(k)
    levels = np.array([10, -10, 5, -5, 0])
    if k % 512:
        return np.exp2(np.random.permutation(np.resize(levels, k // 32))).repeat(32)
    a = np.empty((k // 512, 16))
    for p in range(k // 512):
        a[p, :8] = np.random.permutation(np.resize(levels, 8))
        for g in range(8):
            far = levels[np.abs(levels - a[p, g]) >= 10]
            a[p, g + 8] = far[np.random.randint(len(far))]
    return np.exp2(a.ravel()).repeat(32)


def f64(x):
    return np.asarray(x).astype(np.float64)


def striped(idx):
    return np.tile(idx.reshape(-1, 16).T, (8, 1)).astype(np.uint16)


def unstriped(offs):
    return offs[:16].T.reshape(-1).astype(np.int64)


E2M1 = np.array([0.0, 0.5, 1.0, 1.5, 2.0, 3.0, 4.0, 6.0, -0.0, -0.5, -1.0, -1.5, -2.0, -3.0, -4.0, -6.0])


def pack_weight(w, fmt):
    k, n = w.shape
    w = f64(np.asarray(w, np.float32).astype(ml_dtypes.bfloat16)).reshape(k // 32, 32, n)
    amax = np.abs(w).max(1)
    if fmt == "e4m3":
        byte = np.frexp(amax)[1] - 1 + 127 - 7
    else:
        mant, ex = np.frexp(amax / 6.0)
        byte = np.where(mant > 0.5, ex, ex - 1) + 127
    byte = np.clip(np.where(amax > 0, byte, 1), 1, 254)
    scaled = (w * np.exp2(127.0 - byte)[:, None, :]).reshape(k, n).astype(np.float32)
    by_word = np.ascontiguousarray(scaled.reshape(k // 512, 128, 4, n).transpose(0, 1, 3, 2))
    if fmt == "e4m3":
        words = by_word.astype(ml_dtypes.float8_e4m3fn).view(np.uint8)
    else:
        c = by_word.astype(ml_dtypes.float4_e2m1fn).view(np.uint8) & 0xF
        words = (c[..., 0::2] | (c[..., 1::2] << 4)).reshape(k // 512, 128, 2 * n)
    return np.ascontiguousarray(words), np.ascontiguousarray(byte.astype(np.uint8).reshape(k // 512, 16, n))


def unpack_weight(words, scales, fmt):
    g, _, n = scales.shape
    words = np.ascontiguousarray(words).reshape(g, 128, n, -1)
    if fmt == "e4m3":
        vals = words.view(ml_dtypes.float8_e4m3fn).astype(np.float64)
    else:
        nib = np.empty((g, 128, n, 4), np.uint8)
        nib[..., 0::2] = words & 0xF
        nib[..., 1::2] = words >> 4
        vals = E2M1[nib]
    vals = vals * np.repeat(np.exp2(scales.astype(np.float64) - 127.0), 8, axis=1)[..., None]
    return vals.transpose(0, 1, 3, 2).reshape(g * 512, n)


def gelu(v):
    return 0.5 * v * (1.0 + np.tanh(np.sqrt(2.0 / np.pi) * (v + 0.044715 * v**3)))


def bf(x):
    return np.asarray(x, np.float32).astype(ml_dtypes.bfloat16)


def planes(Y):
    n, m = Y.shape
    b = f64(bf(Y)).reshape(n // 32, 32, m)
    amax = np.abs(b).max(1)
    byte = np.clip(np.where(amax > 0, np.frexp(amax)[1] - 1 + 127 - 7, 1), 1, 254)
    codes = (b * np.exp2(127.0 - byte)[:, None, :]).reshape(n, m).astype(np.float32).astype(ml_dtypes.float8_e4m3fn).view(np.uint8)
    words = codes.reshape(n // 512, 128, 4, m).transpose(0, 1, 3, 2)
    return np.ascontiguousarray(words), np.ascontiguousarray(byte.astype(np.uint8).reshape(n // 512, 16, m))


T, S, P, K, KA, H, N = 4096, 1024, 512, 1024, 512, 1024, 512

def setup_inputs():
    n = np.random.standard_normal
    s = mx_kscale(K)[:, None]
    u = mx_kscale(H)[:, None]
    d = np.exp(0.8 * n((N, 1)))
    tab_words, tab_scales = pack_weight(n((K, T)) * s, "e4m3")
    w2_words, w2_scales = pack_weight(n((K - KA, H)) / np.sqrt(K) / s[KA:], "e2m1")
    wb_words, wb_scales = pack_weight(n((H, N)) / np.sqrt(H) / u, "e4m3")
    return {
        "tab_words": tab_words, "tab_scales": tab_scales,
        "offs": striped(np.random.permutation(T)[:S]),
        "pos1": striped(np.random.permutation(S)[:P]),
        "pos2": striped(np.random.permutation(S)[:P]),
        "w1": (n((KA, H)) / np.sqrt(K) / s[:KA]).astype(np.float32),
        "w2_words": w2_words, "w2_scales": w2_scales,
        "w3": (n((K, H)) / np.sqrt(K) / s).astype(np.float32),
        "gh": (1.3 * np.exp(0.3 * n(H))).astype(np.float32),
        "ma": (n((H, P)) * u).astype(np.float32),
        "gb": (1.2 * np.exp(0.3 * n(H)) * u[:, 0]).astype(np.float32),
        "wa": (n((H, N)) / np.sqrt(H) / u * d.T).astype(np.float32),
        "wb_words": wb_words, "wb_scales": wb_scales,
        "res": (0.7 * n((N, P)) * d).astype(np.float32),
    }

def reference(tab_words, tab_scales, offs, pos1, pos2, w1, w2_words, w2_scales, w3,
              gh, ma, gb, wa, wb_words, wb_scales, res):
    v = unpack_weight(tab_words, tab_scales, "e4m3")[:, unstriped(offs)]
    w2 = unpack_weight(w2_words, w2_scales, "e2m1")
    wb = unpack_weight(wb_words, wb_scales, "e4m3")
    parts = mxq(f64(w1), 0, "e4m3").T @ v[:KA] + w2.T @ v[KA:]
    whole = mxq(f64(w3), 0, "e4m3").T @ v
    h = f64(gh)[:, None] * np.maximum(parts, whole)
    xa = f64(ma) * h[:, unstriped(pos1)]
    xb = f64(gb)[:, None] * np.tanh(h[:, unstriped(pos2)])
    ya = mxq(f64(wa), 0, "e4m3").T @ mxq(xa, 0, "e4m3")
    yb = wb.T @ mxq(xb, 0, "e4m3")
    y = ya * yb + f64(res)
    words, scales = planes(y)
    return y, words, scales

@@ -1,0 +1,386 @@
+from contextlib import ExitStack
+
+import concourse.mybir as mybir
+
+T, S, M, K, H, N = 4096, 1024, 512, 1024, 1024, 512
+FLOPS = 2 * (2 * K * H * S + 2 * H * N * M)
+
+F32 = mybir.dt.float32
+BF16 = mybir.dt.bfloat16
+I32 = mybir.dt.int32
+U32 = mybir.dt.uint32
+U16 = mybir.dt.uint16
+U8 = mybir.dt.uint8
+FP8X4 = mybir.dt.float8_e4m3fn_x4
+FP4X4 = mybir.dt.float4_e2m1fn_x4
+ALU = mybir.AluOpType
+ACT = mybir.ActivationFunctionType
+
+P = 128
+PACK = 4
+PASS = P * PACK
+BANK = 512
+HALF = M // 2
+SLICES = H // P
+EARLY_ROW = 4
+
+
+def tile_list_core_penumbra_reading_kernel(
+    tc, tab_words, tab_scales, offs, pos1, pos2, w1, w2_words, w2_scales, w3,
+    gh, ma, gb, wa, wb_words, wb_scales, res, out_0, out_1, out_2,
+):
+    nc = tc.nc
+    with ExitStack() as ctx:
+        lists = ctx.enter_context(tc.tile_pool(name="lists", bufs=1))
+        sb = ctx.enter_context(tc.tile_pool(name="sb", bufs=1))
+        ps = ctx.enter_context(tc.psum_pool(name="ps", bufs=1))
+
+        def tile(name, shape, dtype):
+            return sb.tile(shape, dtype, name=name, align_bytes=64)
+
+        def tiles(name, count, shape, dtype):
+            return [tile("%s%d" % (name, i), shape, dtype) for i in range(count)]
+
+        offs_t = lists.tile([P, S // 16], U16, name="offs_t")
+        pos1_t = lists.tile([P, M // 16], U16, name="pos1_t")
+        pos2_t = lists.tile([P, M // 16], U16, name="pos2_t")
+
+        tab_w = tiles("tab_w", 2, [P, T], I32)
+        tab_s = tile("tab_s", [P, T], U8)
+        v_w = tiles("v_w", 2, [P, S], U32)
+        v_s = tile("v_s", [P, S], U8)
+        raw = tiles("raw", 3, [P, PACK, PASS], F32)
+        woven = tiles("woven", 3, [P, PACK * PASS], BF16)
+        w_codes = tiles("w_codes", 8, [P, PASS], U32)
+        w_scales = tiles("w_scales", 8, [P, PASS], U8)
+        w2_raw = tile("w2_raw", [P, 2 * H], U8)
+        w2_w = tile("w2_w", [P, 2 * H], U8)
+        w2_sraw = tile("w2_sraw", [P, H], U8)
+        w2_s = tile("w2_s", [P, H], U8)
+        wb_raw = tile("wb_raw", [P, 2 * N], I32)
+        wb_w = tile("wb_w", [P, 2 * N], I32)
+        wb_sraw = tile("wb_sraw", [P, 2 * N], U8)
+        wb_s = tile("wb_s", [P, 2 * N], U8)
+        gh_t = tile("gh_t", [P, SLICES], F32)
+        gb_t = tile("gb_t", [P, SLICES], F32)
+        ma_t = tiles("ma_t", 4, [P, 2 * M], F32)
+        mag = tiles("mag", 4, [P, M], F32)
+        bent = tiles("bent", 2, [P, M], F32)
+        whole_lo = tiles("whole_lo", 2, [P, BANK], F32)
+        whole_hi = tiles("whole_hi", 2, [P, BANK], F32)
+        top = tiles("top", 4, [P, S], F32)
+        xa_first = tile("xa_first", [P, PACK * M], F32)
+        xa_half = tiles("xa_half", 2, [P, PACK * HALF], F32)
+        pick_last = tile("pick_last", [P, PACK * HALF], F32)
+        xb_first = tile("xb_first", [P, PACK * M], BF16)
+        xb_half = tiles("xb_half", 2, [P, PACK * HALF], BF16)
+        xa_codes = tiles("xa_codes", 2, [P, M], U32)
+        xa_scales = tiles("xa_scales", 2, [P, M], U8)
+        xb_codes = tiles("xb_codes", 2, [P, M], U32)
+        xb_scales = tiles("xb_scales", 2, [P, M], U8)
+        res_t = tiles("res_t", 2, [P, PACK * HALF], F32)
+        y_t = tiles("y_t", 2, [P, PACK * HALF], F32)
+        y_codes = tiles("y_codes", 2, [P, HALF], U32)
+        y_scales = tile("y_scales", [P, M], U8)
+        banks = [ps.tile([P, BANK], F32, name="bank%d" % i) for i in range(8)]
+
+        def load_scale_rows(queue, plane, first_row, rows):
+            for q in range(4):
+                queue.dma_start(
+                    out=plane[32 * q + first_row : 32 * q + first_row + 4, :].bitcast(I32),
+                    in_=rows[4 * q : 4 * q + 4, :].bitcast(I32),
+                )
+
+        def load_weight(slot, weight, a, b):
+            nc.sync.dma_start(
+                out=raw[slot][:],
+                in_=weight[a * PASS : (a + 1) * PASS, b * PASS : (b + 1) * PASS].rearrange("(p j) c -> p j c", j=PACK),
+            )
+
+        def load_ma(u):
+            rows = ma[(u // 2) * PASS : (u // 2 + 1) * PASS, :].rearrange("(p t) m -> p t m", t=PACK)
+            nc.sync.dma_start(
+                out=ma_t[u][:].rearrange("p (t m) -> p t m", t=2),
+                in_=rows[:, 2 * (u % 2) : 2 * (u % 2) + 2, :],
+            )
+
+        for plane in (w2_sraw, tab_s, wb_sraw):
+            nc.vector.memset(plane[:].bitcast(I32), 0)
+        load_scale_rows(nc.gpsimd, tab_s, EARLY_ROW, tab_scales[0])
+        load_scale_rows(nc.gpsimd, tab_s, 0, tab_scales[1])
+
+        nc.sync.dma_start(offs_t[:], offs)
+        nc.sync.dma_start(out=w2_raw[:].bitcast(I32), in_=w2_words[0].bitcast(I32))
+        for a in range(2):
+            nc.sync.dma_start(out=tab_w[a][:], in_=tab_words[a].rearrange("p t i -> p (t i)").bitcast(I32))
+        load_scale_rows(nc.sync, w2_sraw, 0, w2_scales[0])
+        load_weight(0, w3, 0, 0)
+        load_weight(1, w3, 1, 0)
+        load_weight(2, w1, 0, 0)
+        nc.sync.dma_start(pos1_t[:], pos1)
+        nc.sync.dma_start(pos2_t[:], pos2)
+        for vec_t, vec in ((gh_t, gh), (gb_t, gb)):
+            nc.sync.dma_start(
+                out=vec_t[:].rearrange("p (b t) -> p b t", t=PACK),
+                in_=vec.rearrange("(b p t) -> p b t", p=P, t=PACK),
+            )
+        load_ma(0)
+        load_ma(1)
+
+        def round_weight(engine_copy, slot, m0, m1):
+            engine_copy(
+                out=woven[slot][:].rearrange("p (t m j) -> p m j t", t=PACK, j=PACK)[:, m0:m1],
+                in_=raw[slot][:].rearrange("p j (m t) -> p m j t", t=PACK)[:, m0:m1],
+            )
+
+        def round_weight_on_scalar(slot):
+            for m0 in (0, P // 2):
+                round_weight(nc.scalar.copy, slot, m0, m0 + P // 2)
+
+        def quantize(codes, scales, src):
+            nc.vector.quantize_mx(out=codes.bitcast(FP8X4), scales=scales, in_=src)
+
+        def quantize_weight(slot, c):
+            quantize(w_codes[c][:], w_scales[c][:], woven[slot][:])
+
+        def weave(engine_copy, dst, src):
+            engine_copy(
+                out=dst.rearrange("p (c i t) -> p c t i", i=PACK, t=PACK),
+                in_=src.rearrange("p (t c i) -> p c t i", i=PACK, t=PACK),
+            )
+
+        def table_pass(out, a, j, lhsT, lhsT_scale, start, stop):
+            cols = slice(j * BANK, (j + 1) * BANK)
+            first_row = EARLY_ROW if a == 0 else 0
+            nc.tensor.matmul_mx(
+                out=out, lhsT=lhsT, lhsT_scale=lhsT_scale,
+                rhs=v_w[a][:, cols].bitcast(FP8X4), rhs_scale=v_s[first_row:P, cols],
+                start=start, stop=stop,
+            )
+
+        def whole_product(i):
+            b, t = divmod(i, PACK)
+            cols = slice(t * P, (t + 1) * P)
+            for j, dst in enumerate((whole_lo, whole_hi)):
+                bank = banks[4 * (i % 2) + j]
+                for a in range(2):
+                    c = 3 * b + a
+                    table_pass(bank[:], a, j, w_codes[c][:, cols].bitcast(FP8X4), w_scales[c][:, cols], a == 0, a == 1)
+                nc.scalar.copy(out=dst[i % 2][:], in_=bank[:])
+
+        def parts_product(i):
+            b, t = divmod(i, PACK)
+            cols = slice(t * P, (t + 1) * P)
+            c = 3 * b + 2
+            for j in range(2):
+                bank = banks[4 * (i % 2) + 2 + j]
+                table_pass(bank[:], 1, j, w2_w[:, 2 * i * P : 2 * (i + 1) * P].bitcast(FP4X4),
+                           w2_s[:, i * P : (i + 1) * P], True, False)
+                table_pass(bank[:], 0, j, w_codes[c][:, cols].bitcast(FP8X4), w_scales[c][:, cols], False, True)
+
+        def take_max(i):
+            for j, src in enumerate((whole_lo, whole_hi)):
+                nc.vector.tensor_tensor(
+                    out=top[i % 4][:, j * BANK : (j + 1) * BANK],
+                    in0=banks[4 * (i % 2) + 2 + j][:], in1=src[i % 2][:], op=ALU.max,
+                )
+
+        def mag_tile(i):
+            return mag[i % 2] if i < 6 else mag[i - 4]
+
+        def scale_rows(out, in0, column):
+            nc.gpsimd.tensor_scalar(out=out, in0=in0, scalar1=column, scalar2=0.0, op0=ALU.mult, op1=ALU.add)
+
+        def scale_ma(i):
+            scale_rows(mag_tile(i)[:], ma_t[i // 2][:, (i % 2) * M : (i % 2 + 1) * M], gh_t[:, i : i + 1])
+
+        def pick_core(i, out, m0, m1):
+            nc.vector.tensor_tensor(
+                out, top[i % 4][:].indirect(pos1_t[:, m0 // 16 : m1 // 16]), mag_tile(i)[:, m0:m1], ALU.mult,
+            )
+
+        def pick_penumbra(i, picked, tanh_out, out, m0, m1):
+            nc.vector.tensor_copy(picked, top[i % 4][:].indirect(pos2_t[:, m0 // 16 : m1 // 16]))
+            nc.scalar.activation(out=tanh_out, in_=picked, func=ACT.Tanh, scale=gh_t[:, i : i + 1])
+            scale_rows(out, tanh_out, gb_t[:, i : i + 1])
+
+        nc.vector.tensor_copy(
+            out=w2_w[:].rearrange("p (b t m r) -> p b t m r", b=2, t=PACK, r=2),
+            in_=w2_raw[:].rearrange("p (b m t r) -> p b t m r", b=2, t=PACK, r=2),
+        )
+        nc.vector.tensor_copy(v_w[0][:], tab_w[0][:].bitcast(U32).indirect(offs_t[:]))
+        nc.vector.tensor_copy(v_s[:], tab_s[:].indirect(offs_t[:]))
+        nc.vector.tensor_copy(v_w[1][:], tab_w[1][:].bitcast(U32).indirect(offs_t[:]))
+        nc.vector.tensor_copy(
+            out=w2_s[:].rearrange("p (b t m) -> p b t m", b=2, t=PACK),
+            in_=w2_sraw[:].rearrange("p (b m t) -> p b t m", b=2, t=PACK),
+        )
+
+        round_weight_on_scalar(0)
+        quantize_weight(0, 0)
+        load_weight(0, w3, 0, 1)
+        round_weight(nc.vector.tensor_copy, 1, 0, P)
+        quantize_weight(1, 1)
+        load_weight(1, w3, 1, 1)
+        whole_product(0)
+        whole_product(1)
+        for engine_copy, t0 in ((nc.vector.tensor_copy, 0), (nc.scalar.copy, 2)):
+            engine_copy(
+                out=woven[2][:].rearrange("p (t m j) -> p m j t", t=PACK, j=PACK)[:, :, :, t0 : t0 + 2],
+                in_=raw[2][:].rearrange("p j (m t) -> p m j t", t=PACK)[:, :, :, t0 : t0 + 2],
+            )
+            quantize(w_codes[2][:, t0 * P : (t0 + 2) * P], w_scales[2][:, t0 * P : (t0 + 2) * P],
+                     woven[2][:, t0 * PASS : (t0 + 2) * PASS])
+        load_weight(2, w1, 0, 1)
+        load_ma(2)
+        load_ma(3)
+        nc.sync.dma_start(
+            out=wb_raw[:].rearrange("p (a c) -> p a c", a=2),
+            in_=wb_words.rearrange("a p c i -> p a (c i)").bitcast(I32),
+        )
+        for q in range(4):
+            nc.sync.dma_start(
+                out=wb_sraw[32 * q : 32 * q + 4, :].bitcast(I32).rearrange("p (a c) -> p a c", a=2),
+                in_=wb_scales[:, 4 * q : 4 * q + 4, :].bitcast(I32).rearrange("a q c -> q a c"),
+            )
+        parts_product(0)
+        parts_product(1)
+        scale_ma(0)
+        scale_ma(1)
+        take_max(0)
+        whole_product(2)
+
+        def after_slice(i):
+            if i < 3:
+                round_weight_on_scalar(i)
+                quantize_weight(i, 3 + i)
+                if i < 2:
+                    load_weight(i, wa, i, 0)
+                else:
+                    for hm in range(2):
+                        nc.sync.dma_start(
+                            out=res_t[hm][:].rearrange("p (t m) -> p t m", t=PACK),
+                            in_=res.rearrange("(p t) m -> p t m", t=PACK)[:, :, hm * HALF : (hm + 1) * HALF],
+                        )
+            if i == 3:
+                weave(nc.scalar.copy, woven[2][:], xa_first[:])
+                quantize(xa_codes[0][:], xa_scales[0][:], woven[2][:])
+            if i == 4:
+                round_weight_on_scalar(0)
+                quantize_weight(0, 6)
+                nc.vector.tensor_copy(
+                    out=wb_w[:].rearrange("p (a t m) -> p a m t", a=2, t=PACK),
+                    in_=wb_raw[:].rearrange("p (a m t) -> p a m t", a=2, t=PACK),
+                )
+            if i == 5:
+                weave(nc.scalar.copy, woven[2][:], xb_first[:])
+                quantize(xb_codes[0][:], xb_scales[0][:], woven[2][:])
+                nc.vector.tensor_copy(
+                    out=wb_s[:].rearrange("p (a t m) -> p a t m", a=2, t=PACK),
+                    in_=wb_sraw[:].rearrange("p (a m t) -> p a t m", a=2, t=PACK),
+                )
+            if i == 6:
+                round_weight_on_scalar(1)
+                quantize_weight(1, 7)
+
+        for i in range(SLICES):
+            t = i % PACK
+            width = M if i < PACK else HALF
+            xa_dst = xa_first if i < PACK else xa_half[0]
+            xb_dst = xb_first if i < PACK else xb_half[0]
+            slot = slice(t * width, (t + 1) * width)
+            pick_core(i, xa_dst[:, slot], 0, width)
+            if i + 2 < 6:
+                scale_ma(i + 2)
+            if i + 1 < SLICES:
+                take_max(i + 1)
+            tanh_tile = mag[i - 1] if i in (3, 4) else bent[i % 2]
+            pick_penumbra(i, whole_hi[(i + 1) % 2][:, 0:width], tanh_tile[:, 0:width], xb_dst[:, slot], 0, width)
+            if i in (3, 4):
+                scale_ma(i + 3)
+            if i + 3 < SLICES and i != 1:
+                whole_product(i + 3)
+            after_slice(i)
+            if i == 1:
+                whole_product(i + 3)
+            if i + 2 < SLICES:
+                parts_product(i + 2)
+
+        quarter = PACK * HALF
+
+        def quantize_half(codes, scales, hm, src):
+            cols = slice(hm * HALF, (hm + 1) * HALF)
+            quantize(codes[1][:, cols], scales[1][:, cols], src)
+
+        def second_product(hm, first_bank, stationary, codes, scales):
+            cols = slice(hm * HALF, (hm + 1) * HALF)
+            for t in range(PACK):
+                out = banks[first_bank + t // 2][:, (t % 2) * HALF : (t % 2 + 1) * HALF]
+                for a in range(2):
+                    lhsT, lhsT_scale = stationary(a, t)
+                    nc.tensor.matmul_mx(
+                        out=out, lhsT=lhsT, lhsT_scale=lhsT_scale,
+                        rhs=codes[a][:, cols].bitcast(FP8X4), rhs_scale=scales[a][:, cols],
+                        start=(a == 0), stop=(a == 1),
+                    )
+
+        def wa_part(a, t):
+            cols = slice(t * P, (t + 1) * P)
+            return w_codes[6 + a][:, cols].bitcast(FP8X4), w_scales[6 + a][:, cols]
+
+        def wb_part(a, t):
+            cols = slice(a * N + t * P, a * N + (t + 1) * P)
+            return wb_w[:, cols].bitcast(FP8X4), wb_s[:, cols]
+
+        def penumbra_product(hm, staged):
+            second_product(hm, 4 * hm, wb_part, xb_codes, xb_scales)
+            for u in range(2):
+                nc.scalar.copy(out=staged[u][:], in_=banks[4 * hm + u][:])
+
+        def finish(hm, staged):
+            for u in range(2):
+                nc.vector.tensor_tensor(out=y_t[hm][:, u * BANK : (u + 1) * BANK], in0=banks[4 * hm + 2 + u][:],
+                                        in1=staged[u][:], op=ALU.mult)
+            for u in range(2):
+                part = y_t[hm][:, u * BANK : (u + 1) * BANK]
+                nc.vector.tensor_tensor(out=part, in0=part, in1=res_t[hm][:, u * BANK : (u + 1) * BANK], op=ALU.add)
+                nc.sync.dma_start(
+                    out=out_0.rearrange("(p t) m -> p t m", t=PACK)[:, 2 * u : 2 * u + 2, hm * HALF : (hm + 1) * HALF],
+                    in_=part.rearrange("p (t m) -> p t m", t=2),
+                )
+
+        def planes(hm, engine_copy, rounded):
+            weave(engine_copy, rounded, y_t[hm][:])
+            quantize(y_codes[hm][:], y_scales[:, hm * HALF : (hm + 1) * HALF], rounded)
+            nc.sync.dma_start(
+                out=out_1[0].rearrange("p m t -> p (m t)").bitcast(I32)[:, hm * HALF : (hm + 1) * HALF],
+                in_=y_codes[hm][:].bitcast(I32),
+            )
+
+        weave(nc.scalar.copy, woven[0][:, 0:quarter], xa_half[0][:])
+        weave(nc.scalar.copy, woven[0][:, quarter:], xb_half[0][:])
+        for t in range(PACK):
+            slot = slice(t * HALF, (t + 1) * HALF)
+            pick_penumbra(PACK + t, pick_last[:, slot], bent[t % 2][:, 0:HALF], xb_half[1][:, slot], HALF, M)
+        quantize_half(xa_codes, xa_scales, 0, woven[0][:, 0:quarter])
+        quantize_half(xb_codes, xb_scales, 0, woven[0][:, quarter:])
+        penumbra_product(0, whole_lo)
+        second_product(0, 2, wa_part, xa_codes, xa_scales)
+        weave(nc.scalar.copy, woven[2][:, 0:quarter], xb_half[1][:])
+        for t in range(PACK):
+            pick_core(PACK + t, xa_half[1][:, t * HALF : (t + 1) * HALF], HALF, M)
+        quantize_half(xb_codes, xb_scales, 1, woven[2][:, 0:quarter])
+        penumbra_product(1, whole_hi)
+        weave(nc.vector.tensor_copy, woven[2][:, quarter:], xa_half[1][:])
+        finish(0, whole_lo)
+        quantize_half(xa_codes, xa_scales, 1, woven[2][:, quarter:])
+        second_product(1, 6, wa_part, xa_codes, xa_scales)
+        planes(0, nc.scalar.copy, woven[1][:, 0:quarter])
+        finish(1, whole_hi)
+        planes(1, nc.vector.tensor_copy, woven[1][:, quarter:])
+        for q in range(4):
+            queue = nc.sync if q % 2 == 0 else nc.scalar
+            queue.dma_start(
+                out=out_2[0][4 * q : 4 * q + 4, :].bitcast(I32),
+                in_=y_scales[32 * q : 32 * q + 4, :].bitcast(I32),
+            )

@@ -20,7 +20,7 @@ P = 128
 PACK = 4
 PASS = P * PACK
 BANK = 512
-HALF = M // 2
+PIECES = ((0, 256), (256, 384), (384, 512))
 SLICES = H // P
 EARLY_ROW = 4
 
@@ -33,6 +33,7 @@ def tile_list_core_penumbra_reading_kernel(
     with ExitStack() as ctx:
         lists = ctx.enter_context(tc.tile_pool(name="lists", bufs=1))
         sb = ctx.enter_context(tc.tile_pool(name="sb", bufs=1))
+        turns = ctx.enter_context(tc.tile_pool(name="turns", bufs=1))
         ps = ctx.enter_context(tc.psum_pool(name="ps", bufs=1))
 
         def tile(name, shape, dtype):
@@ -41,46 +42,52 @@ def tile_list_core_penumbra_reading_kernel(
         def tiles(name, count, shape, dtype):
             return [tile("%s%d" % (name, i), shape, dtype) for i in range(count)]
 
+        def placed(name, kib, shape, dtype):
+            return turns.tile(shape, dtype, name=name, offset=kib * 1024, align_bytes=64)
+
         offs_t = lists.tile([P, S // 16], U16, name="offs_t")
         pos1_t = lists.tile([P, M // 16], U16, name="pos1_t")
         pos2_t = lists.tile([P, M // 16], U16, name="pos2_t")
 
-        tab_w = tiles("tab_w", 2, [P, T], I32)
-        tab_s = tile("tab_s", [P, T], U8)
-        v_w = tiles("v_w", 2, [P, S], U32)
+        tab_w = [placed("tab_w%d" % a, 16 * a, [P, T], I32) for a in range(2)]
+        tab_s = placed("tab_s", 56, [P, T], U8)
+        v_w = [tile("v_w0", [P, S], U32), placed("v_w1", 56, [P, S], U32)]
         v_s = tile("v_s", [P, S], U8)
-        raw = tiles("raw", 3, [P, PACK, PASS], F32)
+        raw = [placed("raw%d" % c, kib, [P, PACK, PASS], F32) for c, kib in enumerate((32, 40, 48, 0, 8, 16, 32, 40))]
         woven = tiles("woven", 3, [P, PACK * PASS], BF16)
+        woven += [placed("woven%d" % c, 48 + 4 * c, [P, PACK * PASS], BF16) for c in (3, 4)]
         w_codes = tiles("w_codes", 8, [P, PASS], U32)
         w_scales = tiles("w_scales", 8, [P, PASS], U8)
         w2_raw = tile("w2_raw", [P, 2 * H], U8)
         w2_w = tile("w2_w", [P, 2 * H], U8)
         w2_sraw = tile("w2_sraw", [P, H], U8)
         w2_s = tile("w2_s", [P, H], U8)
-        wb_raw = tile("wb_raw", [P, 2 * N], I32)
+        wb_raw = placed("wb_raw", 48, [P, 2 * N], I32)
         wb_w = tile("wb_w", [P, 2 * N], I32)
         wb_sraw = tile("wb_sraw", [P, 2 * N], U8)
         wb_s = tile("wb_s", [P, 2 * N], U8)
         gh_t = tile("gh_t", [P, SLICES], F32)
         gb_t = tile("gb_t", [P, SLICES], F32)
-        ma_t = tiles("ma_t", 4, [P, 2 * M], F32)
-        mag = tiles("mag", 4, [P, M], F32)
+        ma_t = tiles("ma_t", 2, [P, 2 * M], F32) + [placed("ma_late%d" % u, 24 + 4 * u, [P, 2 * M], F32) for u in range(2)]
+        mag = tiles("mag", 2, [P, M], F32)
         bent = tiles("bent", 2, [P, M], F32)
-        whole_lo = tiles("whole_lo", 2, [P, BANK], F32)
-        whole_hi = tiles("whole_hi", 2, [P, BANK], F32)
-        top = tiles("top", 4, [P, S], F32)
-        xa_first = tile("xa_first", [P, PACK * M], F32)
-        xa_half = tiles("xa_half", 2, [P, PACK * HALF], F32)
-        pick_last = tile("pick_last", [P, PACK * HALF], F32)
+        whole_lo = tiles("whole_lo", 4, [P, BANK], F32)
+        whole_hi = [tile("whole_hi0", [P, BANK], F32), placed("whole_hi1", 72, [P, BANK], F32)]
+        top = tiles("top", 3, [P, S], F32) + [placed("top3", 62, [P, S], F32)]
+        xa_wide = tile("xa_wide", [P, (PACK + 1) * M], F32)
+        xa_first = xa_wide[:, 0 : PACK * M]
+        late = [placed("late%d" % u, 72 + 4 * u, [P, 2 * M], F32) for u in range(2)]
+        xa_piece = [tile("xa_piece0", [P, 2 * M], F32)[:], late[0][:, 0:M], late[1][:, 0:M]]
+        bent_piece = [tile("bent_piece0", [P, 2 * M], F32)[:], late[0][:, M:], late[1][:, M:]]
+        woven_first = placed("woven_first", 76, [P, PACK * M], BF16)
+        woven.append(xa_wide[:, 3 * M : 5 * M].bitcast(BF16))
         xb_first = tile("xb_first", [P, PACK * M], BF16)
-        xb_half = tiles("xb_half", 2, [P, PACK * HALF], BF16)
         xa_codes = tiles("xa_codes", 2, [P, M], U32)
         xa_scales = tiles("xa_scales", 2, [P, M], U8)
         xb_codes = tiles("xb_codes", 2, [P, M], U32)
         xb_scales = tiles("xb_scales", 2, [P, M], U8)
-        res_t = tiles("res_t", 2, [P, PACK * HALF], F32)
-        y_t = tiles("y_t", 2, [P, PACK * HALF], F32)
-        y_codes = tiles("y_codes", 2, [P, HALF], U32)
+        y_t = [placed("y_t%d" % k, kib, [P, PACK * (m1 - m0)], F32) for k, (kib, (m0, m1)) in enumerate(zip((52, 0, 2), PIECES))]
+        y_codes = [tile("y_codes%d" % k, [P, m1 - m0], U32) for k, (m0, m1) in enumerate(PIECES)]
         y_scales = tile("y_scales", [P, M], U8)
         banks = [ps.tile([P, BANK], F32, name="bank%d" % i) for i in range(8)]
 
@@ -104,19 +111,18 @@ def tile_list_core_penumbra_reading_kernel(
                 in_=rows[:, 2 * (u % 2) : 2 * (u % 2) + 2, :],
             )
 
-        for plane in (w2_sraw, tab_s, wb_sraw):
+        for plane in (tab_s, w2_sraw, wb_sraw):
             nc.vector.memset(plane[:].bitcast(I32), 0)
         load_scale_rows(nc.gpsimd, tab_s, EARLY_ROW, tab_scales[0])
         load_scale_rows(nc.gpsimd, tab_s, 0, tab_scales[1])
 
+        def table_words(a):
+            return tab_words[a].rearrange("p t i -> p (t i)").bitcast(I32)
+
         nc.sync.dma_start(offs_t[:], offs)
+        for c0 in (0, T // 2):
+            nc.sync.dma_start(out=tab_w[0][:, c0 : c0 + T // 2], in_=table_words(0)[:, c0 : c0 + T // 2])
         nc.sync.dma_start(out=w2_raw[:].bitcast(I32), in_=w2_words[0].bitcast(I32))
-        for a in range(2):
-            nc.sync.dma_start(out=tab_w[a][:], in_=tab_words[a].rearrange("p t i -> p (t i)").bitcast(I32))
-        load_scale_rows(nc.sync, w2_sraw, 0, w2_scales[0])
-        load_weight(0, w3, 0, 0)
-        load_weight(1, w3, 1, 0)
-        load_weight(2, w1, 0, 0)
         nc.sync.dma_start(pos1_t[:], pos1)
         nc.sync.dma_start(pos2_t[:], pos2)
         for vec_t, vec in ((gh_t, gh), (gb_t, gb)):
@@ -124,18 +130,19 @@ def tile_list_core_penumbra_reading_kernel(
                 out=vec_t[:].rearrange("p (b t) -> p b t", t=PACK),
                 in_=vec.rearrange("(b p t) -> p b t", p=P, t=PACK),
             )
+        nc.sync.dma_start(out=tab_w[1][:], in_=table_words(1))
+        load_weight(0, w3, 0, 0)
+        load_scale_rows(nc.sync, w2_sraw, 0, w2_scales[0])
+        load_weight(1, w3, 1, 0)
+        load_weight(2, w1, 0, 0)
         load_ma(0)
         load_ma(1)
 
-        def round_weight(engine_copy, slot, m0, m1):
-            engine_copy(
-                out=woven[slot][:].rearrange("p (t m j) -> p m j t", t=PACK, j=PACK)[:, m0:m1],
-                in_=raw[slot][:].rearrange("p j (m t) -> p m j t", t=PACK)[:, m0:m1],
+        def round_weight_on_scalar(slot, c):
+            nc.scalar.copy(
+                out=woven[slot][:].rearrange("p (t m j) -> p m j t", t=PACK, j=PACK),
+                in_=raw[c][:].rearrange("p j (m t) -> p m j t", t=PACK),
             )
-
-        def round_weight_on_scalar(slot):
-            for m0 in (0, P // 2):
-                round_weight(nc.scalar.copy, slot, m0, m0 + P // 2)
 
         def quantize(codes, scales, src):
             nc.vector.quantize_mx(out=codes.bitcast(FP8X4), scales=scales, in_=src)
@@ -166,7 +173,7 @@ def tile_list_core_penumbra_reading_kernel(
                 for a in range(2):
                     c = 3 * b + a
                     table_pass(bank[:], a, j, w_codes[c][:, cols].bitcast(FP8X4), w_scales[c][:, cols], a == 0, a == 1)
-                nc.scalar.copy(out=dst[i % 2][:], in_=bank[:])
+                nc.scalar.copy(out=dst[i % len(dst)][:], in_=bank[:])
 
         def parts_product(i):
             b, t = divmod(i, PACK)
@@ -182,58 +189,71 @@ def tile_list_core_penumbra_reading_kernel(
             for j, src in enumerate((whole_lo, whole_hi)):
                 nc.vector.tensor_tensor(
                     out=top[i % 4][:, j * BANK : (j + 1) * BANK],
-                    in0=banks[4 * (i % 2) + 2 + j][:], in1=src[i % 2][:], op=ALU.max,
+                    in0=banks[4 * (i % 2) + 2 + j][:], in1=src[i % len(src)][:], op=ALU.max,
                 )
 
-        def mag_tile(i):
-            return mag[i % 2] if i < 6 else mag[i - 4]
+        def gained_ma(i):
+            if i < 6:
+                return ma_t[0][:, (i % 2) * M : (i % 2 + 1) * M]
+            return mag[i % 2][:]
 
         def scale_rows(out, in0, column):
             nc.gpsimd.tensor_scalar(out=out, in0=in0, scalar1=column, scalar2=0.0, op0=ALU.mult, op1=ALU.add)
 
         def scale_ma(i):
-            scale_rows(mag_tile(i)[:], ma_t[i // 2][:, (i % 2) * M : (i % 2 + 1) * M], gh_t[:, i : i + 1])
+            src = ma_t[i // 2][:, (i % 2) * M : (i % 2 + 1) * M]
+            if i in (2, 3, 4, 5, 6):
+                scale_rows(gained_ma(i), src, gh_t[:, i : i + 1])
+            else:
+                nc.scalar.activation(out=gained_ma(i), in_=src, func=ACT.Copy, scale=gh_t[:, i : i + 1])
 
         def pick_core(i, out, m0, m1):
             nc.vector.tensor_tensor(
-                out, top[i % 4][:].indirect(pos1_t[:, m0 // 16 : m1 // 16]), mag_tile(i)[:, m0:m1], ALU.mult,
+                out, top[i % 4][:].indirect(pos1_t[:, m0 // 16 : m1 // 16]), gained_ma(i)[:, m0:m1], ALU.mult,
             )
 
-        def pick_penumbra(i, picked, tanh_out, out, m0, m1):
+        def pick_penumbra(i, picked, tanh_out, m0, m1):
             nc.vector.tensor_copy(picked, top[i % 4][:].indirect(pos2_t[:, m0 // 16 : m1 // 16]))
             nc.scalar.activation(out=tanh_out, in_=picked, func=ACT.Tanh, scale=gh_t[:, i : i + 1])
-            scale_rows(out, tanh_out, gb_t[:, i : i + 1])
 
+        def weave_scaled(dst, src, gains):
+            shape = [P, src.shape[1] // (PACK * PACK), PACK, PACK]
+            nc.vector.tensor_tensor(
+                out=dst.rearrange("p (c i t) -> p c t i", i=PACK, t=PACK),
+                in0=src.rearrange("p (t c i) -> p c t i", i=PACK, t=PACK),
+                in1=gains.unsqueeze(1).unsqueeze(3).to_broadcast(shape), op=ALU.mult,
+            )
+
+        def round_weight_shared(slot, c, second_copy):
+            for engine_copy, t0 in ((nc.vector.tensor_copy, 0), (second_copy, 2)):
+                engine_copy(
+                    out=woven[slot][:].rearrange("p (t m j) -> p m j t", t=PACK, j=PACK)[:, :, :, t0 : t0 + 2],
+                    in_=raw[c][:].rearrange("p j (m t) -> p m j t", t=PACK)[:, :, :, t0 : t0 + 2],
+                )
+                quantize(w_codes[c][:, t0 * P : (t0 + 2) * P], w_scales[c][:, t0 * P : (t0 + 2) * P],
+                         woven[slot][:, t0 * PASS : (t0 + 2) * PASS])
+
+        nc.vector.tensor_copy(v_w[0][:], tab_w[0][:].bitcast(U32).indirect(offs_t[:]))
         nc.vector.tensor_copy(
             out=w2_w[:].rearrange("p (b t m r) -> p b t m r", b=2, t=PACK, r=2),
             in_=w2_raw[:].rearrange("p (b m t r) -> p b t m r", b=2, t=PACK, r=2),
         )
-        nc.vector.tensor_copy(v_w[0][:], tab_w[0][:].bitcast(U32).indirect(offs_t[:]))
         nc.vector.tensor_copy(v_s[:], tab_s[:].indirect(offs_t[:]))
         nc.vector.tensor_copy(v_w[1][:], tab_w[1][:].bitcast(U32).indirect(offs_t[:]))
         nc.vector.tensor_copy(
             out=w2_s[:].rearrange("p (b t m) -> p b t m", b=2, t=PACK),
             in_=w2_sraw[:].rearrange("p (b m t) -> p b t m", b=2, t=PACK),
         )
-
-        round_weight_on_scalar(0)
-        quantize_weight(0, 0)
-        load_weight(0, w3, 0, 1)
-        round_weight(nc.vector.tensor_copy, 1, 0, P)
-        quantize_weight(1, 1)
-        load_weight(1, w3, 1, 1)
-        whole_product(0)
-        whole_product(1)
-        for engine_copy, t0 in ((nc.vector.tensor_copy, 0), (nc.scalar.copy, 2)):
-            engine_copy(
-                out=woven[2][:].rearrange("p (t m j) -> p m j t", t=PACK, j=PACK)[:, :, :, t0 : t0 + 2],
-                in_=raw[2][:].rearrange("p j (m t) -> p m j t", t=PACK)[:, :, :, t0 : t0 + 2],
-            )
-            quantize(w_codes[2][:, t0 * P : (t0 + 2) * P], w_scales[2][:, t0 * P : (t0 + 2) * P],
-                     woven[2][:, t0 * PASS : (t0 + 2) * PASS])
-        load_weight(2, w1, 0, 1)
+        load_weight(3, w3, 0, 1)
+        load_weight(4, w3, 1, 1)
+        load_weight(5, w1, 0, 1)
         load_ma(2)
         load_ma(3)
+        round_weight_shared(0, 0, nc.scalar.copy)
+        round_weight_shared(1, 1, nc.scalar.copy)
+        round_weight_shared(2, 2, nc.vector.tensor_copy)
+        load_weight(6, wa, 0, 0)
+        load_weight(7, wa, 1, 0)
         nc.sync.dma_start(
             out=wb_raw[:].rearrange("p (a c) -> p a c", a=2),
             in_=wb_words.rearrange("a p c i -> p a (c i)").bitcast(I32),
@@ -243,84 +263,85 @@ def tile_list_core_penumbra_reading_kernel(
                 out=wb_sraw[32 * q : 32 * q + 4, :].bitcast(I32).rearrange("p (a c) -> p a c", a=2),
                 in_=wb_scales[:, 4 * q : 4 * q + 4, :].bitcast(I32).rearrange("a q c -> q a c"),
             )
+        whole_product(0)
         parts_product(0)
-        parts_product(1)
         scale_ma(0)
+        whole_product(1)
+        parts_product(1)
         scale_ma(1)
         take_max(0)
         whole_product(2)
+        round_weight_on_scalar(3, 3)
+        quantize_weight(3, 3)
 
         def after_slice(i):
-            if i < 3:
-                round_weight_on_scalar(i)
-                quantize_weight(i, 3 + i)
-                if i < 2:
-                    load_weight(i, wa, i, 0)
-                else:
-                    for hm in range(2):
-                        nc.sync.dma_start(
-                            out=res_t[hm][:].rearrange("p (t m) -> p t m", t=PACK),
-                            in_=res.rearrange("(p t) m -> p t m", t=PACK)[:, :, hm * HALF : (hm + 1) * HALF],
-                        )
+            if i == 0:
+                round_weight_on_scalar(4, 4)
+                quantize_weight(4, 4)
+                for k, (m0, m1) in enumerate(PIECES):
+                    nc.sync.dma_start(
+                        out=y_t[k][:].rearrange("p (t m) -> p t m", t=PACK),
+                        in_=res.rearrange("(p t) m -> p t m", t=PACK)[:, :, m0:m1],
+                    )
+            if i == 2:
+                scale_ma(7)
+                round_weight_on_scalar(0, 6)
+                quantize_weight(0, 6)
             if i == 3:
+                scale_ma(6)
                 weave(nc.scalar.copy, woven[2][:], xa_first[:])
                 quantize(xa_codes[0][:], xa_scales[0][:], woven[2][:])
             if i == 4:
-                round_weight_on_scalar(0)
-                quantize_weight(0, 6)
+                round_weight_on_scalar(1, 7)
+                quantize_weight(1, 7)
                 nc.vector.tensor_copy(
                     out=wb_w[:].rearrange("p (a t m) -> p a m t", a=2, t=PACK),
                     in_=wb_raw[:].rearrange("p (a m t) -> p a m t", a=2, t=PACK),
                 )
             if i == 5:
-                weave(nc.scalar.copy, woven[2][:], xb_first[:])
-                quantize(xb_codes[0][:], xb_scales[0][:], woven[2][:])
+                weave(nc.scalar.copy, woven[0][:], xb_first[:])
+                quantize(xb_codes[0][:], xb_scales[0][:], woven[0][:])
                 nc.vector.tensor_copy(
                     out=wb_s[:].rearrange("p (a t m) -> p a t m", a=2, t=PACK),
                     in_=wb_sraw[:].rearrange("p (a m t) -> p a t m", a=2, t=PACK),
                 )
-            if i == 6:
-                round_weight_on_scalar(1)
-                quantize_weight(1, 7)
 
         for i in range(SLICES):
             t = i % PACK
-            width = M if i < PACK else HALF
-            xa_dst = xa_first if i < PACK else xa_half[0]
-            xb_dst = xb_first if i < PACK else xb_half[0]
+            width = M if i < PACK else PIECES[0][1]
             slot = slice(t * width, (t + 1) * width)
-            pick_core(i, xa_dst[:, slot], 0, width)
-            if i + 2 < 6:
+            pick_core(i, (xa_first if i < PACK else xa_piece[0])[:, slot], 0, width)
+            if i < PACK:
                 scale_ma(i + 2)
+            if i == 2:
+                round_weight_on_scalar(5, 5)
+                quantize_weight(5, 5)
+                whole_product(4)
             if i + 1 < SLICES:
                 take_max(i + 1)
-            tanh_tile = mag[i - 1] if i in (3, 4) else bent[i % 2]
-            pick_penumbra(i, whole_hi[(i + 1) % 2][:, 0:width], tanh_tile[:, 0:width], xb_dst[:, slot], 0, width)
-            if i in (3, 4):
-                scale_ma(i + 3)
+            picked = whole_lo[(i + 1) % 4][:, 0:width]
+            if i < PACK:
+                tanh_tile = mag[0] if i == 3 else bent[i % 2]
+                pick_penumbra(i, picked, tanh_tile[:], 0, width)
+                scale_rows(xb_first[:, slot], tanh_tile[:], gb_t[:, i : i + 1])
+            else:
+                pick_penumbra(i, picked, bent_piece[0][:, slot], 0, width)
             if i + 3 < SLICES and i != 1:
                 whole_product(i + 3)
             after_slice(i)
-            if i == 1:
-                whole_product(i + 3)
             if i + 2 < SLICES:
                 parts_product(i + 2)
 
-        quarter = PACK * HALF
-
-        def quantize_half(codes, scales, hm, src):
-            cols = slice(hm * HALF, (hm + 1) * HALF)
-            quantize(codes[1][:, cols], scales[1][:, cols], src)
-
-        def second_product(hm, first_bank, stationary, codes, scales):
-            cols = slice(hm * HALF, (hm + 1) * HALF)
+        def second_product(k, first_bank, stationary, codes, scales):
+            m0, m1 = PIECES[k]
+            per_bank = BANK // (m1 - m0)
             for t in range(PACK):
-                out = banks[first_bank + t // 2][:, (t % 2) * HALF : (t % 2 + 1) * HALF]
+                out = banks[first_bank + t // per_bank][:, (t % per_bank) * (m1 - m0) : (t % per_bank + 1) * (m1 - m0)]
                 for a in range(2):
                     lhsT, lhsT_scale = stationary(a, t)
                     nc.tensor.matmul_mx(
                         out=out, lhsT=lhsT, lhsT_scale=lhsT_scale,
-                        rhs=codes[a][:, cols].bitcast(FP8X4), rhs_scale=scales[a][:, cols],
+                        rhs=codes[a][:, m0:m1].bitcast(FP8X4), rhs_scale=scales[a][:, m0:m1],
                         start=(a == 0), stop=(a == 1),
                     )
 
@@ -332,52 +353,68 @@ def tile_list_core_penumbra_reading_kernel(
             cols = slice(a * N + t * P, a * N + (t + 1) * P)
             return wb_w[:, cols].bitcast(FP8X4), wb_s[:, cols]
 
-        def penumbra_product(hm, staged):
-            second_product(hm, 4 * hm, wb_part, xb_codes, xb_scales)
-            for u in range(2):
-                nc.scalar.copy(out=staged[u][:], in_=banks[4 * hm + u][:])
+        yb_bank = (0, 4, 6)
+        ya_bank = (2, 5, 7)
+        staged = ((whole_lo[1], whole_lo[2]), (whole_lo[3],), (whole_hi[0],))
 
-        def finish(hm, staged):
-            for u in range(2):
-                nc.vector.tensor_tensor(out=y_t[hm][:, u * BANK : (u + 1) * BANK], in0=banks[4 * hm + 2 + u][:],
-                                        in1=staged[u][:], op=ALU.mult)
-            for u in range(2):
-                part = y_t[hm][:, u * BANK : (u + 1) * BANK]
-                nc.vector.tensor_tensor(out=part, in0=part, in1=res_t[hm][:, u * BANK : (u + 1) * BANK], op=ALU.add)
-                nc.sync.dma_start(
-                    out=out_0.rearrange("(p t) m -> p t m", t=PACK)[:, 2 * u : 2 * u + 2, hm * HALF : (hm + 1) * HALF],
-                    in_=part.rearrange("p (t m) -> p t m", t=2),
-                )
+        def span(k):
+            return slice(PACK * PIECES[k][0], PACK * PIECES[k][1])
 
-        def planes(hm, engine_copy, rounded):
-            weave(engine_copy, rounded, y_t[hm][:])
-            quantize(y_codes[hm][:], y_scales[:, hm * HALF : (hm + 1) * HALF], rounded)
+        def pick_piece(k):
+            m0, m1 = PIECES[k]
+            for t in range(PACK):
+                part = bent_piece[k][:, t * (m1 - m0) : (t + 1) * (m1 - m0)]
+                pick_penumbra(PACK + t, part, part, m0, m1)
+            for t in range(PACK):
+                pick_core(PACK + t, xa_piece[k][:, t * (m1 - m0) : (t + 1) * (m1 - m0)], m0, m1)
+
+        def multiply_piece(k, engine_copy):
+            m0, m1 = PIECES[k]
+            xa_woven = woven_first[:, 0 : 2 * M] if k == 0 else woven[2][:, span(k)]
+            xb_woven = woven_first[:, 2 * M :] if k == 0 else woven[1][:, span(k)]
+            weave(engine_copy, xa_woven, xa_piece[k][:])
+            if k == 1:
+                rounded = xb_first[:, span(k)]
+                for t in range(PACK):
+                    slot = slice(t * (m1 - m0), (t + 1) * (m1 - m0))
+                    nc.scalar.activation(out=rounded[:, slot], in_=bent_piece[k][:, slot], func=ACT.Copy,
+                                         scale=gb_t[:, PACK + t : PACK + t + 1])
+                weave(nc.scalar.copy, xb_woven, rounded)
+            else:
+                weave_scaled(xb_woven, bent_piece[k][:], gb_t[:, PACK:])
+            quantize(xb_codes[1][:, m0:m1], xb_scales[1][:, m0:m1], xb_woven)
+            quantize(xa_codes[1][:, m0:m1], xa_scales[1][:, m0:m1], xa_woven)
+            second_product(k, yb_bank[k], wb_part, xb_codes, xb_scales)
+            second_product(k, ya_bank[k], wa_part, xa_codes, xa_scales)
+            for u, dst in enumerate(staged[k]):
+                nc.scalar.copy(out=dst[:], in_=banks[yb_bank[k] + u][:])
+
+        def finish_piece(k, engine_copy):
+            m0, m1 = PIECES[k]
+            for u, part in enumerate(staged[k]):
+                nc.vector.tensor_tensor(out=part[:], in0=banks[ya_bank[k] + u][:], in1=part[:], op=ALU.mult)
+            for u, part in enumerate(staged[k]):
+                rows = y_t[k][:, u * BANK : (u + 1) * BANK]
+                nc.vector.tensor_tensor(out=rows, in0=rows, in1=part[:], op=ALU.add)
             nc.sync.dma_start(
-                out=out_1[0].rearrange("p m t -> p (m t)").bitcast(I32)[:, hm * HALF : (hm + 1) * HALF],
-                in_=y_codes[hm][:].bitcast(I32),
+                out=out_0.rearrange("(p t) m -> p t m", t=PACK)[:, :, m0:m1],
+                in_=y_t[k][:].rearrange("p (t m) -> p t m", t=PACK),
+            )
+            weave(engine_copy, woven[0][:, span(k)], y_t[k][:])
+            quantize(y_codes[k][:], y_scales[:, m0:m1], woven[0][:, span(k)])
+            nc.sync.dma_start(
+                out=out_1[0].rearrange("p m t -> p (m t)").bitcast(I32)[:, m0:m1],
+                in_=y_codes[k][:].bitcast(I32),
             )
 
-        weave(nc.scalar.copy, woven[0][:, 0:quarter], xa_half[0][:])
-        weave(nc.scalar.copy, woven[0][:, quarter:], xb_half[0][:])
-        for t in range(PACK):
-            slot = slice(t * HALF, (t + 1) * HALF)
-            pick_penumbra(PACK + t, pick_last[:, slot], bent[t % 2][:, 0:HALF], xb_half[1][:, slot], HALF, M)
-        quantize_half(xa_codes, xa_scales, 0, woven[0][:, 0:quarter])
-        quantize_half(xb_codes, xb_scales, 0, woven[0][:, quarter:])
-        penumbra_product(0, whole_lo)
-        second_product(0, 2, wa_part, xa_codes, xa_scales)
-        weave(nc.scalar.copy, woven[2][:, 0:quarter], xb_half[1][:])
-        for t in range(PACK):
-            pick_core(PACK + t, xa_half[1][:, t * HALF : (t + 1) * HALF], HALF, M)
-        quantize_half(xb_codes, xb_scales, 1, woven[2][:, 0:quarter])
-        penumbra_product(1, whole_hi)
-        weave(nc.vector.tensor_copy, woven[2][:, quarter:], xa_half[1][:])
-        finish(0, whole_lo)
-        quantize_half(xa_codes, xa_scales, 1, woven[2][:, quarter:])
-        second_product(1, 6, wa_part, xa_codes, xa_scales)
-        planes(0, nc.scalar.copy, woven[1][:, 0:quarter])
-        finish(1, whole_hi)
-        planes(1, nc.vector.tensor_copy, woven[1][:, quarter:])
+        multiply_piece(0, nc.scalar.copy)
+        pick_piece(1)
+        multiply_piece(1, nc.scalar.copy)
+        pick_piece(2)
+        multiply_piece(2, nc.vector.tensor_copy)
+        finish_piece(0, nc.scalar.copy)
+        finish_piece(1, nc.scalar.copy)
+        finish_piece(2, nc.vector.tensor_copy)
         for q in range(4):
             queue = nc.sync if q % 2 == 0 else nc.scalar
             queue.dma_start(

@@ -91,8 +91,8 @@ def tile_list_core_penumbra_reading_kernel(
         y_scales = tile("y_scales", [P, M], U8)
         banks = [ps.tile([P, BANK], F32, name="bank%d" % i) for i in range(8)]
 
-        def load_scale_rows(queue, plane, first_row, rows):
-            for q in range(4):
+        def load_scale_rows(queues, plane, first_row, rows):
+            for q, queue in enumerate(queues):
                 queue.dma_start(
                     out=plane[32 * q + first_row : 32 * q + first_row + 4, :].bitcast(I32),
                     in_=rows[4 * q : 4 * q + 4, :].bitcast(I32),
@@ -113,16 +113,13 @@ def tile_list_core_penumbra_reading_kernel(
 
         for plane in (tab_s, w2_sraw, wb_sraw):
             nc.vector.memset(plane[:].bitcast(I32), 0)
-        load_scale_rows(nc.gpsimd, tab_s, EARLY_ROW, tab_scales[0])
-        load_scale_rows(nc.gpsimd, tab_s, 0, tab_scales[1])
 
-        def table_words(a):
-            return tab_words[a].rearrange("p t i -> p (t i)").bitcast(I32)
+        def load_table_words(a, c0, c1):
+            words = tab_words[a].rearrange("p t i -> p (t i)").bitcast(I32)
+            nc.sync.dma_start(out=tab_w[a][:, c0:c1], in_=words[:, c0:c1])
 
         nc.sync.dma_start(offs_t[:], offs)
-        for c0 in (0, T // 2):
-            nc.sync.dma_start(out=tab_w[0][:, c0 : c0 + T // 2], in_=table_words(0)[:, c0 : c0 + T // 2])
-        nc.sync.dma_start(out=w2_raw[:].bitcast(I32), in_=w2_words[0].bitcast(I32))
+        load_table_words(0, 0, T // 2)
         nc.sync.dma_start(pos1_t[:], pos1)
         nc.sync.dma_start(pos2_t[:], pos2)
         for vec_t, vec in ((gh_t, gh), (gb_t, gb)):
@@ -130,9 +127,13 @@ def tile_list_core_penumbra_reading_kernel(
                 out=vec_t[:].rearrange("p (b t) -> p b t", t=PACK),
                 in_=vec.rearrange("(b p t) -> p b t", p=P, t=PACK),
             )
-        nc.sync.dma_start(out=tab_w[1][:], in_=table_words(1))
+        nc.sync.dma_start(out=w2_raw[:].bitcast(I32), in_=w2_words[0].bitcast(I32))
+        load_table_words(0, T // 2, T)
+        load_scale_rows((nc.gpsimd, nc.sync, nc.sync, nc.sync), tab_s, EARLY_ROW, tab_scales[0])
+        load_scale_rows((nc.gpsimd, nc.sync, nc.sync, nc.sync), tab_s, 0, tab_scales[1])
+        load_table_words(1, 0, T)
         load_weight(0, w3, 0, 0)
-        load_scale_rows(nc.sync, w2_sraw, 0, w2_scales[0])
+        load_scale_rows((nc.sync,) * 4, w2_sraw, 0, w2_scales[0])
         load_weight(1, w3, 1, 0)
         load_weight(2, w1, 0, 0)
         load_ma(0)
@@ -294,9 +295,9 @@ def tile_list_core_penumbra_reading_kernel(
             if i == 4:
                 round_weight_on_scalar(1, 7)
                 quantize_weight(1, 7)
-                nc.vector.tensor_copy(
-                    out=wb_w[:].rearrange("p (a t m) -> p a m t", a=2, t=PACK),
-                    in_=wb_raw[:].rearrange("p (a m t) -> p a m t", a=2, t=PACK),
+                nc.scalar.copy(
+                    out=wb_w[:].bitcast(U32).rearrange("p (a t m) -> p a m t", a=2, t=PACK),
+                    in_=wb_raw[:].bitcast(U32).rearrange("p (a m t) -> p a m t", a=2, t=PACK),
                 )
             if i == 5:
                 weave(nc.scalar.copy, woven[0][:], xb_first[:])

@@ -69,8 +69,7 @@ def tile_list_core_penumbra_reading_kernel(
         gh_t = tile("gh_t", [P, SLICES], F32)
         gb_t = tile("gb_t", [P, SLICES], F32)
         ma_t = tiles("ma_t", 2, [P, 2 * M], F32) + [placed("ma_late%d" % u, 24 + 4 * u, [P, 2 * M], F32) for u in range(2)]
-        mag = tiles("mag", 2, [P, M], F32)
-        bent = tiles("bent", 2, [P, M], F32)
+        bent_first = tile("bent_first", [P, PACK * M], F32)
         whole_lo = tiles("whole_lo", 4, [P, BANK], F32)
         whole_hi = [tile("whole_hi0", [P, BANK], F32), placed("whole_hi1", 72, [P, BANK], F32)]
         top = tiles("top", 3, [P, S], F32) + [placed("top3", 62, [P, S], F32)]
@@ -87,15 +86,15 @@ def tile_list_core_penumbra_reading_kernel(
         xb_codes = tiles("xb_codes", 2, [P, M], U32)
         xb_scales = tiles("xb_scales", 2, [P, M], U8)
         y_t = [placed("y_t%d" % k, kib, [P, PACK * (m1 - m0)], F32) for k, (kib, (m0, m1)) in enumerate(zip((52, 0, 2), PIECES))]
-        y_codes = [tile("y_codes%d" % k, [P, m1 - m0], U32) for k, (m0, m1) in enumerate(PIECES)]
+        y_codes = tile("y_codes", [P, M], U32)
         y_scales = tile("y_scales", [P, M], U8)
         banks = [ps.tile([P, BANK], F32, name="bank%d" % i) for i in range(8)]
 
-        def load_scale_rows(queues, plane, first_row, rows):
-            for q, queue in enumerate(queues):
-                queue.dma_start(
-                    out=plane[32 * q + first_row : 32 * q + first_row + 4, :].bitcast(I32),
-                    in_=rows[4 * q : 4 * q + 4, :].bitcast(I32),
+        def load_scale_rows(plane, first_row, rows):
+            for r in range(4):
+                nc.sync.dma_start(
+                    out=plane[first_row + r : P : 32, :].bitcast(I32),
+                    in_=rows[r : 16 : 4, :].bitcast(I32),
                 )
 
         def load_weight(slot, weight, a, b):
@@ -129,11 +128,11 @@ def tile_list_core_penumbra_reading_kernel(
             )
         nc.sync.dma_start(out=w2_raw[:].bitcast(I32), in_=w2_words[0].bitcast(I32))
         load_table_words(0, T // 2, T)
-        load_scale_rows((nc.gpsimd, nc.sync, nc.sync, nc.sync), tab_s, EARLY_ROW, tab_scales[0])
-        load_scale_rows((nc.gpsimd, nc.sync, nc.sync, nc.sync), tab_s, 0, tab_scales[1])
+        load_scale_rows(tab_s, EARLY_ROW, tab_scales[0])
+        load_scale_rows(tab_s, 0, tab_scales[1])
         load_table_words(1, 0, T)
         load_weight(0, w3, 0, 0)
-        load_scale_rows((nc.sync,) * 4, w2_sraw, 0, w2_scales[0])
+        load_scale_rows(w2_sraw, 0, w2_scales[0])
         load_weight(1, w3, 1, 0)
         load_weight(2, w1, 0, 0)
         load_ma(0)
@@ -193,24 +192,22 @@ def tile_list_core_penumbra_reading_kernel(
                     in0=banks[4 * (i % 2) + 2 + j][:], in1=src[i % len(src)][:], op=ALU.max,
                 )
 
-        def gained_ma(i):
-            if i < 6:
-                return ma_t[0][:, (i % 2) * M : (i % 2 + 1) * M]
-            return mag[i % 2][:]
-
-        def scale_rows(out, in0, column):
-            nc.gpsimd.tensor_scalar(out=out, in0=in0, scalar1=column, scalar2=0.0, op0=ALU.mult, op1=ALU.add)
+        def ma_slice(i):
+            return ma_t[i // 2][:, (i % 2) * M : (i % 2 + 1) * M]
 
         def scale_ma(i):
-            src = ma_t[i // 2][:, (i % 2) * M : (i % 2 + 1) * M]
-            if i in (2, 3, 4, 5, 6):
-                scale_rows(gained_ma(i), src, gh_t[:, i : i + 1])
-            else:
-                nc.scalar.activation(out=gained_ma(i), in_=src, func=ACT.Copy, scale=gh_t[:, i : i + 1])
+            nc.scalar.activation(out=ma_slice(i), in_=ma_slice(i), func=ACT.Copy, scale=gh_t[:, i : i + 1])
+
+        def scale_bent(rounded, bent, b):
+            width = bent.shape[1] // PACK
+            for t in range(PACK):
+                slot = slice(t * width, (t + 1) * width)
+                nc.scalar.activation(out=rounded[:, slot], in_=bent[:, slot], func=ACT.Copy,
+                                     scale=gb_t[:, PACK * b + t : PACK * b + t + 1])
 
         def pick_core(i, out, m0, m1):
             nc.vector.tensor_tensor(
-                out, top[i % 4][:].indirect(pos1_t[:, m0 // 16 : m1 // 16]), gained_ma(i)[:, m0:m1], ALU.mult,
+                out, top[i % 4][:].indirect(pos1_t[:, m0 // 16 : m1 // 16]), ma_slice(i)[:, m0:m1], ALU.mult,
             )
 
         def pick_penumbra(i, picked, tanh_out, m0, m1):
@@ -259,10 +256,10 @@ def tile_list_core_penumbra_reading_kernel(
             out=wb_raw[:].rearrange("p (a c) -> p a c", a=2),
             in_=wb_words.rearrange("a p c i -> p a (c i)").bitcast(I32),
         )
-        for q in range(4):
+        for r in range(4):
             nc.sync.dma_start(
-                out=wb_sraw[32 * q : 32 * q + 4, :].bitcast(I32).rearrange("p (a c) -> p a c", a=2),
-                in_=wb_scales[:, 4 * q : 4 * q + 4, :].bitcast(I32).rearrange("a q c -> q a c"),
+                out=wb_sraw[r : P : 32, :].bitcast(I32).rearrange("p (a c) -> p a c", a=2),
+                in_=wb_scales[:, r : 16 : 4, :].bitcast(I32).rearrange("a q c -> q a c"),
             )
         whole_product(0)
         parts_product(0)
@@ -274,6 +271,7 @@ def tile_list_core_penumbra_reading_kernel(
         whole_product(2)
         round_weight_on_scalar(3, 3)
         quantize_weight(3, 3)
+        scale_ma(2)
 
         def after_slice(i):
             if i == 0:
@@ -285,23 +283,27 @@ def tile_list_core_penumbra_reading_kernel(
                         in_=res.rearrange("(p t) m -> p t m", t=PACK)[:, :, m0:m1],
                     )
             if i == 2:
-                scale_ma(7)
+                scale_ma(4)
+                scale_ma(5)
                 round_weight_on_scalar(0, 6)
                 quantize_weight(0, 6)
             if i == 3:
                 scale_ma(6)
+                scale_ma(7)
                 weave(nc.scalar.copy, woven[2][:], xa_first[:])
                 quantize(xa_codes[0][:], xa_scales[0][:], woven[2][:])
             if i == 4:
+                scale_bent(xb_first[:], bent_first[:], 0)
+                weave(nc.vector.tensor_copy, woven[0][:], xb_first[:])
                 round_weight_on_scalar(1, 7)
+            if i == 5:
+                quantize(xb_codes[0][:], xb_scales[0][:], woven[0][:])
                 quantize_weight(1, 7)
                 nc.scalar.copy(
                     out=wb_w[:].bitcast(U32).rearrange("p (a t m) -> p a m t", a=2, t=PACK),
                     in_=wb_raw[:].bitcast(U32).rearrange("p (a m t) -> p a m t", a=2, t=PACK),
                 )
-            if i == 5:
-                weave(nc.scalar.copy, woven[0][:], xb_first[:])
-                quantize(xb_codes[0][:], xb_scales[0][:], woven[0][:])
+            if i == 6:
                 nc.vector.tensor_copy(
                     out=wb_s[:].rearrange("p (a t m) -> p a t m", a=2, t=PACK),
                     in_=wb_sraw[:].rearrange("p (a m t) -> p a t m", a=2, t=PACK),
@@ -312,21 +314,15 @@ def tile_list_core_penumbra_reading_kernel(
             width = M if i < PACK else PIECES[0][1]
             slot = slice(t * width, (t + 1) * width)
             pick_core(i, (xa_first if i < PACK else xa_piece[0])[:, slot], 0, width)
-            if i < PACK:
-                scale_ma(i + 2)
             if i == 2:
                 round_weight_on_scalar(5, 5)
                 quantize_weight(5, 5)
                 whole_product(4)
+                scale_ma(3)
             if i + 1 < SLICES:
                 take_max(i + 1)
             picked = whole_lo[(i + 1) % 4][:, 0:width]
-            if i < PACK:
-                tanh_tile = mag[0] if i == 3 else bent[i % 2]
-                pick_penumbra(i, picked, tanh_tile[:], 0, width)
-                scale_rows(xb_first[:, slot], tanh_tile[:], gb_t[:, i : i + 1])
-            else:
-                pick_penumbra(i, picked, bent_piece[0][:, slot], 0, width)
+            pick_penumbra(i, picked, (bent_first if i < PACK else bent_piece[0])[:, slot], 0, width)
             if i + 3 < SLICES and i != 1:
                 whole_product(i + 3)
             after_slice(i)
@@ -375,23 +371,19 @@ def tile_list_core_penumbra_reading_kernel(
             xb_woven = woven_first[:, 2 * M :] if k == 0 else woven[1][:, span(k)]
             weave(engine_copy, xa_woven, xa_piece[k][:])
             if k == 1:
-                rounded = xb_first[:, span(k)]
-                for t in range(PACK):
-                    slot = slice(t * (m1 - m0), (t + 1) * (m1 - m0))
-                    nc.scalar.activation(out=rounded[:, slot], in_=bent_piece[k][:, slot], func=ACT.Copy,
-                                         scale=gb_t[:, PACK + t : PACK + t + 1])
-                weave(nc.scalar.copy, xb_woven, rounded)
+                scale_bent(xb_first[:, span(k)], bent_piece[k], 1)
+                weave(nc.scalar.copy, xb_woven, xb_first[:, span(k)])
             else:
                 weave_scaled(xb_woven, bent_piece[k][:], gb_t[:, PACK:])
             quantize(xb_codes[1][:, m0:m1], xb_scales[1][:, m0:m1], xb_woven)
             quantize(xa_codes[1][:, m0:m1], xa_scales[1][:, m0:m1], xa_woven)
             second_product(k, yb_bank[k], wb_part, xb_codes, xb_scales)
             second_product(k, ya_bank[k], wa_part, xa_codes, xa_scales)
-            for u, dst in enumerate(staged[k]):
-                nc.scalar.copy(out=dst[:], in_=banks[yb_bank[k] + u][:])
 
         def finish_piece(k, engine_copy):
             m0, m1 = PIECES[k]
+            for u, part in enumerate(staged[k]):
+                nc.scalar.copy(out=part[:], in_=banks[yb_bank[k] + u][:])
             for u, part in enumerate(staged[k]):
                 nc.vector.tensor_tensor(out=part[:], in0=banks[ya_bank[k] + u][:], in1=part[:], op=ALU.mult)
             for u, part in enumerate(staged[k]):
@@ -402,23 +394,27 @@ def tile_list_core_penumbra_reading_kernel(
                 in_=y_t[k][:].rearrange("p (t m) -> p t m", t=PACK),
             )
             weave(engine_copy, woven[0][:, span(k)], y_t[k][:])
-            quantize(y_codes[k][:], y_scales[:, m0:m1], woven[0][:, span(k)])
+            quantize(y_codes[:, m0:m1], y_scales[:, m0:m1], woven[0][:, span(k)])
+
+        def store_codes(m0, m1):
             nc.sync.dma_start(
                 out=out_1[0].rearrange("p m t -> p (m t)").bitcast(I32)[:, m0:m1],
-                in_=y_codes[k][:].bitcast(I32),
+                in_=y_codes[:, m0:m1].bitcast(I32),
             )
 
         multiply_piece(0, nc.scalar.copy)
         pick_piece(1)
-        multiply_piece(1, nc.scalar.copy)
         pick_piece(2)
+        multiply_piece(1, nc.scalar.copy)
         multiply_piece(2, nc.vector.tensor_copy)
         finish_piece(0, nc.scalar.copy)
         finish_piece(1, nc.scalar.copy)
+        store_codes(0, PIECES[2][0])
         finish_piece(2, nc.vector.tensor_copy)
-        for q in range(4):
-            queue = nc.sync if q % 2 == 0 else nc.scalar
+        store_codes(PIECES[2][0], M)
+        for r in range(4):
+            queue = nc.sync if r % 2 == 0 else nc.scalar
             queue.dma_start(
-                out=out_2[0][4 * q : 4 * q + 4, :].bitcast(I32),
-                in_=y_scales[32 * q : 32 * q + 4, :].bitcast(I32),
+                out=out_2[0][r : 16 : 4, :].bitcast(I32),
+                in_=y_scales[r : P : 32, :].bitcast(I32),
             )

from contextlib import ExitStack

import concourse.mybir as mybir

T, S, M, K, H, N = 4096, 1024, 512, 1024, 1024, 512
FLOPS = 2 * (2 * K * H * S + 2 * H * N * M)

F32 = mybir.dt.float32
BF16 = mybir.dt.bfloat16
I32 = mybir.dt.int32
U32 = mybir.dt.uint32
U16 = mybir.dt.uint16
U8 = mybir.dt.uint8
FP8X4 = mybir.dt.float8_e4m3fn_x4
FP4X4 = mybir.dt.float4_e2m1fn_x4
ALU = mybir.AluOpType
ACT = mybir.ActivationFunctionType

P = 128
PACK = 4
PASS = P * PACK
BANK = 512
PIECES = ((0, 256), (256, 384), (384, 512))
SLICES = H // P
EARLY_ROW = 4


def tile_list_core_penumbra_reading_kernel(
    tc, tab_words, tab_scales, offs, pos1, pos2, w1, w2_words, w2_scales, w3,
    gh, ma, gb, wa, wb_words, wb_scales, res, out_0, out_1, out_2,
):
    nc = tc.nc
    with ExitStack() as ctx:
        lists = ctx.enter_context(tc.tile_pool(name="lists", bufs=1))
        sb = ctx.enter_context(tc.tile_pool(name="sb", bufs=1))
        turns = ctx.enter_context(tc.tile_pool(name="turns", bufs=1))
        ps = ctx.enter_context(tc.psum_pool(name="ps", bufs=1))

        def tile(name, shape, dtype):
            return sb.tile(shape, dtype, name=name, align_bytes=64)

        def tiles(name, count, shape, dtype):
            return [tile("%s%d" % (name, i), shape, dtype) for i in range(count)]

        def placed(name, kib, shape, dtype):
            return turns.tile(shape, dtype, name=name, offset=kib * 1024, align_bytes=64)

        offs_t = lists.tile([P, S // 16], U16, name="offs_t")
        pos1_t = lists.tile([P, M // 16], U16, name="pos1_t")
        pos2_t = lists.tile([P, M // 16], U16, name="pos2_t")

        tab_w = [placed("tab_w%d" % a, 16 * a, [P, T], I32) for a in range(2)]
        tab_s = placed("tab_s", 56, [P, T], U8)
        v_w = [tile("v_w0", [P, S], U32), placed("v_w1", 56, [P, S], U32)]
        v_s = tile("v_s", [P, S], U8)
        raw = [placed("raw%d" % c, kib, [P, PACK, PASS], F32) for c, kib in enumerate((32, 40, 48, 0, 8, 16, 32, 40))]
        woven = tiles("woven", 3, [P, PACK * PASS], BF16)
        woven += [placed("woven%d" % c, 48 + 4 * c, [P, PACK * PASS], BF16) for c in (3, 4)]
        w_codes = tiles("w_codes", 8, [P, PASS], U32)
        w_scales = tiles("w_scales", 8, [P, PASS], U8)
        w2_raw = tile("w2_raw", [P, 2 * H], U8)
        w2_w = tile("w2_w", [P, 2 * H], U8)
        w2_sraw = tile("w2_sraw", [P, H], U8)
        w2_s = tile("w2_s", [P, H], U8)
        wb_raw = placed("wb_raw", 48, [P, 2 * N], I32)
        wb_w = tile("wb_w", [P, 2 * N], I32)
        wb_sraw = tile("wb_sraw", [P, 2 * N], U8)
        wb_s = tile("wb_s", [P, 2 * N], U8)
        gh_t = tile("gh_t", [P, SLICES], F32)
        gb_t = tile("gb_t", [P, SLICES], F32)
        ma_t = tiles("ma_t", 2, [P, 2 * M], F32) + [placed("ma_late%d" % u, 24 + 4 * u, [P, 2 * M], F32) for u in range(2)]
        bent_first = tile("bent_first", [P, PACK * M], F32)
        whole_lo = tiles("whole_lo", 4, [P, BANK], F32)
        whole_hi = [tile("whole_hi0", [P, BANK], F32), placed("whole_hi1", 72, [P, BANK], F32)]
        top = tiles("top", 3, [P, S], F32) + [placed("top3", 62, [P, S], F32)]
        xa_wide = tile("xa_wide", [P, (PACK + 1) * M], F32)
        xa_first = xa_wide[:, 0 : PACK * M]
        late = [placed("late%d" % u, 72 + 4 * u, [P, 2 * M], F32) for u in range(2)]
        xa_piece = [tile("xa_piece0", [P, 2 * M], F32)[:], late[0][:, 0:M], late[1][:, 0:M]]
        bent_piece = [tile("bent_piece0", [P, 2 * M], F32)[:], late[0][:, M:], late[1][:, M:]]
        woven_first = placed("woven_first", 76, [P, PACK * M], BF16)
        woven.append(xa_wide[:, 3 * M : 5 * M].bitcast(BF16))
        xb_first = tile("xb_first", [P, PACK * M], BF16)
        xa_codes = tiles("xa_codes", 2, [P, M], U32)
        xa_scales = tiles("xa_scales", 2, [P, M], U8)
        xb_codes = tiles("xb_codes", 2, [P, M], U32)
        xb_scales = tiles("xb_scales", 2, [P, M], U8)
        y_t = [placed("y_t%d" % k, kib, [P, PACK * (m1 - m0)], F32) for k, (kib, (m0, m1)) in enumerate(zip((52, 0, 2), PIECES))]
        y_codes = tile("y_codes", [P, M], U32)
        y_scales = tile("y_scales", [P, M], U8)
        banks = [ps.tile([P, BANK], F32, name="bank%d" % i) for i in range(8)]

        def load_scale_rows(plane, first_row, rows):
            for r in range(4):
                nc.sync.dma_start(
                    out=plane[first_row + r : P : 32, :].bitcast(I32),
                    in_=rows[r : 16 : 4, :].bitcast(I32),
                )

        def load_weight(slot, weight, a, b):
            nc.sync.dma_start(
                out=raw[slot][:],
                in_=weight[a * PASS : (a + 1) * PASS, b * PASS : (b + 1) * PASS].rearrange("(p j) c -> p j c", j=PACK),
            )

        def load_ma(u):
            rows = ma[(u // 2) * PASS : (u // 2 + 1) * PASS, :].rearrange("(p t) m -> p t m", t=PACK)
            nc.sync.dma_start(
                out=ma_t[u][:].rearrange("p (t m) -> p t m", t=2),
                in_=rows[:, 2 * (u % 2) : 2 * (u % 2) + 2, :],
            )

        for plane in (tab_s, w2_sraw, wb_sraw):
            nc.vector.memset(plane[:].bitcast(I32), 0)

        def load_table_words(a, c0, c1):
            words = tab_words[a].rearrange("p t i -> p (t i)").bitcast(I32)
            nc.sync.dma_start(out=tab_w[a][:, c0:c1], in_=words[:, c0:c1])

        nc.sync.dma_start(offs_t[:], offs)
        load_table_words(0, 0, T // 2)
        nc.sync.dma_start(pos1_t[:], pos1)
        nc.sync.dma_start(pos2_t[:], pos2)
        for vec_t, vec in ((gh_t, gh), (gb_t, gb)):
            nc.sync.dma_start(
                out=vec_t[:].rearrange("p (b t) -> p b t", t=PACK),
                in_=vec.rearrange("(b p t) -> p b t", p=P, t=PACK),
            )
        nc.sync.dma_start(out=w2_raw[:].bitcast(I32), in_=w2_words[0].bitcast(I32))
        load_table_words(0, T // 2, T)
        load_scale_rows(tab_s, EARLY_ROW, tab_scales[0])
        load_scale_rows(tab_s, 0, tab_scales[1])
        load_table_words(1, 0, T)
        load_weight(0, w3, 0, 0)
        load_scale_rows(w2_sraw, 0, w2_scales[0])
        load_weight(1, w3, 1, 0)
        load_weight(2, w1, 0, 0)
        load_ma(0)
        load_ma(1)

        def round_weight_on_scalar(slot, c):
            nc.scalar.copy(
                out=woven[slot][:].rearrange("p (t m j) -> p m j t", t=PACK, j=PACK),
                in_=raw[c][:].rearrange("p j (m t) -> p m j t", t=PACK),
            )

        def quantize(codes, scales, src):
            nc.vector.quantize_mx(out=codes.bitcast(FP8X4), scales=scales, in_=src)

        def quantize_weight(slot, c):
            quantize(w_codes[c][:], w_scales[c][:], woven[slot][:])

        def weave(engine_copy, dst, src):
            engine_copy(
                out=dst.rearrange("p (c i t) -> p c t i", i=PACK, t=PACK),
                in_=src.rearrange("p (t c i) -> p c t i", i=PACK, t=PACK),
            )

        def table_pass(out, a, j, lhsT, lhsT_scale, start, stop):
            cols = slice(j * BANK, (j + 1) * BANK)
            first_row = EARLY_ROW if a == 0 else 0
            nc.tensor.matmul_mx(
                out=out, lhsT=lhsT, lhsT_scale=lhsT_scale,
                rhs=v_w[a][:, cols].bitcast(FP8X4), rhs_scale=v_s[first_row:P, cols],
                start=start, stop=stop,
            )

        def whole_product(i):
            b, t = divmod(i, PACK)
            cols = slice(t * P, (t + 1) * P)
            for j, dst in enumerate((whole_lo, whole_hi)):
                bank = banks[4 * (i % 2) + j]
                for a in range(2):
                    c = 3 * b + a
                    table_pass(bank[:], a, j, w_codes[c][:, cols].bitcast(FP8X4), w_scales[c][:, cols], a == 0, a == 1)
                nc.scalar.copy(out=dst[i % len(dst)][:], in_=bank[:])

        def parts_product(i):
            b, t = divmod(i, PACK)
            cols = slice(t * P, (t + 1) * P)
            c = 3 * b + 2
            for j in range(2):
                bank = banks[4 * (i % 2) + 2 + j]
                table_pass(bank[:], 1, j, w2_w[:, 2 * i * P : 2 * (i + 1) * P].bitcast(FP4X4),
                           w2_s[:, i * P : (i + 1) * P], True, False)
                table_pass(bank[:], 0, j, w_codes[c][:, cols].bitcast(FP8X4), w_scales[c][:, cols], False, True)

        def take_max(i):
            for j, src in enumerate((whole_lo, whole_hi)):
                nc.vector.tensor_tensor(
                    out=top[i % 4][:, j * BANK : (j + 1) * BANK],
                    in0=banks[4 * (i % 2) + 2 + j][:], in1=src[i % len(src)][:], op=ALU.max,
                )

        def ma_slice(i):
            return ma_t[i // 2][:, (i % 2) * M : (i % 2 + 1) * M]

        def scale_ma(i):
            nc.scalar.activation(out=ma_slice(i), in_=ma_slice(i), func=ACT.Copy, scale=gh_t[:, i : i + 1])

        def scale_bent(rounded, bent, b):
            width = bent.shape[1] // PACK
            for t in range(PACK):
                slot = slice(t * width, (t + 1) * width)
                nc.scalar.activation(out=rounded[:, slot], in_=bent[:, slot], func=ACT.Copy,
                                     scale=gb_t[:, PACK * b + t : PACK * b + t + 1])

        def pick_core(i, out, m0, m1):
            nc.vector.tensor_tensor(
                out, top[i % 4][:].indirect(pos1_t[:, m0 // 16 : m1 // 16]), ma_slice(i)[:, m0:m1], ALU.mult,
            )

        def pick_penumbra(i, picked, tanh_out, m0, m1):
            nc.vector.tensor_copy(picked, top[i % 4][:].indirect(pos2_t[:, m0 // 16 : m1 // 16]))
            nc.scalar.activation(out=tanh_out, in_=picked, func=ACT.Tanh, scale=gh_t[:, i : i + 1])

        def weave_scaled(dst, src, gains):
            shape = [P, src.shape[1] // (PACK * PACK), PACK, PACK]
            nc.vector.tensor_tensor(
                out=dst.rearrange("p (c i t) -> p c t i", i=PACK, t=PACK),
                in0=src.rearrange("p (t c i) -> p c t i", i=PACK, t=PACK),
                in1=gains.unsqueeze(1).unsqueeze(3).to_broadcast(shape), op=ALU.mult,
            )

        def round_weight_shared(slot, c, second_copy):
            for engine_copy, t0 in ((nc.vector.tensor_copy, 0), (second_copy, 2)):
                engine_copy(
                    out=woven[slot][:].rearrange("p (t m j) -> p m j t", t=PACK, j=PACK)[:, :, :, t0 : t0 + 2],
                    in_=raw[c][:].rearrange("p j (m t) -> p m j t", t=PACK)[:, :, :, t0 : t0 + 2],
                )
                quantize(w_codes[c][:, t0 * P : (t0 + 2) * P], w_scales[c][:, t0 * P : (t0 + 2) * P],
                         woven[slot][:, t0 * PASS : (t0 + 2) * PASS])

        nc.vector.tensor_copy(v_w[0][:], tab_w[0][:].bitcast(U32).indirect(offs_t[:]))
        nc.vector.tensor_copy(
            out=w2_w[:].rearrange("p (b t m r) -> p b t m r", b=2, t=PACK, r=2),
            in_=w2_raw[:].rearrange("p (b m t r) -> p b t m r", b=2, t=PACK, r=2),
        )
        nc.vector.tensor_copy(v_s[:], tab_s[:].indirect(offs_t[:]))
        nc.vector.tensor_copy(v_w[1][:], tab_w[1][:].bitcast(U32).indirect(offs_t[:]))
        nc.vector.tensor_copy(
            out=w2_s[:].rearrange("p (b t m) -> p b t m", b=2, t=PACK),
            in_=w2_sraw[:].rearrange("p (b m t) -> p b t m", b=2, t=PACK),
        )
        load_weight(3, w3, 0, 1)
        load_weight(4, w3, 1, 1)
        load_weight(5, w1, 0, 1)
        load_ma(2)
        load_ma(3)
        round_weight_shared(0, 0, nc.scalar.copy)
        round_weight_shared(1, 1, nc.scalar.copy)
        round_weight_shared(2, 2, nc.vector.tensor_copy)
        load_weight(6, wa, 0, 0)
        load_weight(7, wa, 1, 0)
        nc.sync.dma_start(
            out=wb_raw[:].rearrange("p (a c) -> p a c", a=2),
            in_=wb_words.rearrange("a p c i -> p a (c i)").bitcast(I32),
        )
        for r in range(4):
            nc.sync.dma_start(
                out=wb_sraw[r : P : 32, :].bitcast(I32).rearrange("p (a c) -> p a c", a=2),
                in_=wb_scales[:, r : 16 : 4, :].bitcast(I32).rearrange("a q c -> q a c"),
            )
        whole_product(0)
        parts_product(0)
        scale_ma(0)
        whole_product(1)
        parts_product(1)
        scale_ma(1)
        take_max(0)
        whole_product(2)
        round_weight_on_scalar(3, 3)
        quantize_weight(3, 3)
        scale_ma(2)

        def after_slice(i):
            if i == 0:
                round_weight_on_scalar(4, 4)
                quantize_weight(4, 4)
                for k, (m0, m1) in enumerate(PIECES):
                    nc.sync.dma_start(
                        out=y_t[k][:].rearrange("p (t m) -> p t m", t=PACK),
                        in_=res.rearrange("(p t) m -> p t m", t=PACK)[:, :, m0:m1],
                    )
            if i == 2:
                scale_ma(4)
                scale_ma(5)
                round_weight_on_scalar(0, 6)
                quantize_weight(0, 6)
            if i == 3:
                scale_ma(6)
                scale_ma(7)
                weave(nc.scalar.copy, woven[2][:], xa_first[:])
                quantize(xa_codes[0][:], xa_scales[0][:], woven[2][:])
            if i == 4:
                scale_bent(xb_first[:], bent_first[:], 0)
                weave(nc.vector.tensor_copy, woven[0][:], xb_first[:])
                round_weight_on_scalar(1, 7)
            if i == 5:
                quantize(xb_codes[0][:], xb_scales[0][:], woven[0][:])
                quantize_weight(1, 7)
                nc.scalar.copy(
                    out=wb_w[:].bitcast(U32).rearrange("p (a t m) -> p a m t", a=2, t=PACK),
                    in_=wb_raw[:].bitcast(U32).rearrange("p (a m t) -> p a m t", a=2, t=PACK),
                )
            if i == 6:
                nc.vector.tensor_copy(
                    out=wb_s[:].rearrange("p (a t m) -> p a t m", a=2, t=PACK),
                    in_=wb_sraw[:].rearrange("p (a m t) -> p a t m", a=2, t=PACK),
                )

        for i in range(SLICES):
            t = i % PACK
            width = M if i < PACK else PIECES[0][1]
            slot = slice(t * width, (t + 1) * width)
            pick_core(i, (xa_first if i < PACK else xa_piece[0])[:, slot], 0, width)
            if i == 2:
                round_weight_on_scalar(5, 5)
                quantize_weight(5, 5)
                whole_product(4)
                scale_ma(3)
            if i + 1 < SLICES:
                take_max(i + 1)
            picked = whole_lo[(i + 1) % 4][:, 0:width]
            pick_penumbra(i, picked, (bent_first if i < PACK else bent_piece[0])[:, slot], 0, width)
            if i + 3 < SLICES and i != 1:
                whole_product(i + 3)
            after_slice(i)
            if i + 2 < SLICES:
                parts_product(i + 2)

        def second_product(k, first_bank, stationary, codes, scales):
            m0, m1 = PIECES[k]
            per_bank = BANK // (m1 - m0)
            for t in range(PACK):
                out = banks[first_bank + t // per_bank][:, (t % per_bank) * (m1 - m0) : (t % per_bank + 1) * (m1 - m0)]
                for a in range(2):
                    lhsT, lhsT_scale = stationary(a, t)
                    nc.tensor.matmul_mx(
                        out=out, lhsT=lhsT, lhsT_scale=lhsT_scale,
                        rhs=codes[a][:, m0:m1].bitcast(FP8X4), rhs_scale=scales[a][:, m0:m1],
                        start=(a == 0), stop=(a == 1),
                    )

        def wa_part(a, t):
            cols = slice(t * P, (t + 1) * P)
            return w_codes[6 + a][:, cols].bitcast(FP8X4), w_scales[6 + a][:, cols]

        def wb_part(a, t):
            cols = slice(a * N + t * P, a * N + (t + 1) * P)
            return wb_w[:, cols].bitcast(FP8X4), wb_s[:, cols]

        yb_bank = (0, 4, 6)
        ya_bank = (2, 5, 7)
        staged = ((whole_lo[1], whole_lo[2]), (whole_lo[3],), (whole_hi[0],))

        def span(k):
            return slice(PACK * PIECES[k][0], PACK * PIECES[k][1])

        def pick_piece(k):
            m0, m1 = PIECES[k]
            for t in range(PACK):
                part = bent_piece[k][:, t * (m1 - m0) : (t + 1) * (m1 - m0)]
                pick_penumbra(PACK + t, part, part, m0, m1)
            for t in range(PACK):
                pick_core(PACK + t, xa_piece[k][:, t * (m1 - m0) : (t + 1) * (m1 - m0)], m0, m1)

        def multiply_piece(k, engine_copy):
            m0, m1 = PIECES[k]
            xa_woven = woven_first[:, 0 : 2 * M] if k == 0 else woven[2][:, span(k)]
            xb_woven = woven_first[:, 2 * M :] if k == 0 else woven[1][:, span(k)]
            weave(engine_copy, xa_woven, xa_piece[k][:])
            if k == 1:
                scale_bent(xb_first[:, span(k)], bent_piece[k], 1)
                weave(nc.scalar.copy, xb_woven, xb_first[:, span(k)])
            else:
                weave_scaled(xb_woven, bent_piece[k][:], gb_t[:, PACK:])
            quantize(xb_codes[1][:, m0:m1], xb_scales[1][:, m0:m1], xb_woven)
            quantize(xa_codes[1][:, m0:m1], xa_scales[1][:, m0:m1], xa_woven)
            second_product(k, yb_bank[k], wb_part, xb_codes, xb_scales)
            second_product(k, ya_bank[k], wa_part, xa_codes, xa_scales)

        def finish_piece(k, engine_copy):
            m0, m1 = PIECES[k]
            for u, part in enumerate(staged[k]):
                nc.scalar.copy(out=part[:], in_=banks[yb_bank[k] + u][:])
            for u, part in enumerate(staged[k]):
                nc.vector.tensor_tensor(out=part[:], in0=banks[ya_bank[k] + u][:], in1=part[:], op=ALU.mult)
            for u, part in enumerate(staged[k]):
                rows = y_t[k][:, u * BANK : (u + 1) * BANK]
                nc.vector.tensor_tensor(out=rows, in0=rows, in1=part[:], op=ALU.add)
            nc.sync.dma_start(
                out=out_0.rearrange("(p t) m -> p t m", t=PACK)[:, :, m0:m1],
                in_=y_t[k][:].rearrange("p (t m) -> p t m", t=PACK),
            )
            weave(engine_copy, woven[0][:, span(k)], y_t[k][:])
            quantize(y_codes[:, m0:m1], y_scales[:, m0:m1], woven[0][:, span(k)])

        def store_codes(m0, m1):
            nc.sync.dma_start(
                out=out_1[0].rearrange("p m t -> p (m t)").bitcast(I32)[:, m0:m1],
                in_=y_codes[:, m0:m1].bitcast(I32),
            )

        multiply_piece(0, nc.scalar.copy)
        pick_piece(1)
        pick_piece(2)
        multiply_piece(1, nc.scalar.copy)
        multiply_piece(2, nc.vector.tensor_copy)
        finish_piece(0, nc.scalar.copy)
        finish_piece(1, nc.scalar.copy)
        store_codes(0, PIECES[2][0])
        finish_piece(2, nc.vector.tensor_copy)
        store_codes(PIECES[2][0], M)
        for r in range(4):
            queue = nc.sync if r % 2 == 0 else nc.scalar
            queue.dma_start(
                out=out_2[0][r : 16 : 4, :].bitcast(I32),
                in_=y_scales[r : P : 32, :].bitcast(I32),
            )
